import numpy as np
import ml_dtypes


def mxq(x, axis, fmt="e4m3"):
    dtype, down = {"e4m3": (ml_dtypes.float8_e4m3fn, 7), "e5m2": (ml_dtypes.float8_e5m2, 14)}[fmt]
    v = np.moveaxis(np.asarray(x, np.float32).astype(ml_dtypes.bfloat16).astype(np.float64), axis, -1)
    blocks = v.reshape(v.shape[:-1] + (-1, 32))
    amax = np.abs(blocks).max(-1, keepdims=True)
    byte = np.maximum(np.where(amax > 0, np.frexp(amax)[1] - 1 + 127, 0) - down, 1)
    scale = np.exp2(byte - 127.0)
    codes = (blocks / scale).astype(np.float32).astype(dtype).astype(np.float64)
    return np.moveaxis((codes * scale).reshape(v.shape), -1, axis)


WIDE = False


def mx_kscale(k):
    if not WIDE:
        return np.ones(k)
    levels = np.array([10, -10, 5, -5, 0])
    if k % 512:
        return np.exp2(np.random.permutation(np.resize(levels, k // 32))).repeat(32)
    a = np.empty((k // 512, 16))
    for p in range(k // 512):
        a[p, :8] = np.random.permutation(np.resize(levels, 8))
        for g in range(8):
            far = levels[np.abs(levels - a[p, g]) >= 10]
            a[p, g + 8] = far[np.random.randint(len(far))]
    return np.exp2(a.ravel()).repeat(32)


def f64(x):
    return np.asarray(x).astype(np.float64)


def striped(idx):
    return np.tile(np.asarray(idx).reshape(-1, 16).T, (8, 1)).astype(np.uint16)


def unstriped(offs):
    return offs[:16].T.reshape(-1).astype(np.int64)


def striped8(idx):
    return np.asarray(idx).reshape(8, -1, 16).transpose(0, 2, 1).reshape(128, -1).astype(np.uint16)


def unstriped8(offs):
    return offs.reshape(8, 16, -1).transpose(0, 2, 1).reshape(8, -1).astype(np.int64)


def pick8(x, idx, run):
    r = np.arange(len(x))
    return x[r[:, None], idx[r % (8 * run) // run]]


E2M1 = np.array([0.0, 0.5, 1.0, 1.5, 2.0, 3.0, 4.0, 6.0, -0.0, -0.5, -1.0, -1.5, -2.0, -3.0, -4.0, -6.0])


def pack_weight(w, fmt):
    k, n = w.shape
    w = f64(np.asarray(w, np.float32).astype(ml_dtypes.bfloat16)).reshape(k // 32, 32, n)
    amax = np.abs(w).max(1)
    if fmt == "e4m3":
        byte = np.frexp(amax)[1] - 1 + 127 - 7
    else:
        mant, ex = np.frexp(amax / 6.0)
        byte = np.where(mant > 0.5, ex, ex - 1) + 127
    byte = np.clip(np.where(amax > 0, byte, 1), 1, 254)
    scaled = (w * np.exp2(127.0 - byte)[:, None, :]).reshape(k, n).astype(np.float32)
    by_word = np.ascontiguousarray(scaled.reshape(k // 512, 128, 4, n).transpose(0, 1, 3, 2))
    if fmt == "e4m3":
        words = by_word.astype(ml_dtypes.float8_e4m3fn).view(np.uint8)
    else:
        c = by_word.astype(ml_dtypes.float4_e2m1fn).view(np.uint8) & 0xF
        words = (c[..., 0::2] | (c[..., 1::2] << 4)).reshape(k // 512, 128, 2 * n)
    return np.ascontiguousarray(words), np.ascontiguousarray(byte.astype(np.uint8).reshape(k // 512, 16, n))


def unpack_weight(words, scales, fmt):
    g, _, n = scales.shape
    words = np.ascontiguousarray(words).reshape(g, 128, n, -1)
    if fmt == "e4m3":
        vals = words.view(ml_dtypes.float8_e4m3fn).astype(np.float64)
    else:
        nib = np.empty((g, 128, n, 4), np.uint8)
        nib[..., 0::2] = words & 0xF
        nib[..., 1::2] = words >> 4
        vals = E2M1[nib]
    vals = vals * np.repeat(np.exp2(scales.astype(np.float64) - 127.0), 8, axis=1)[..., None]
    return vals.transpose(0, 1, 3, 2).reshape(g * 512, n)


K, J, R, T, F, O, C, N, U, E = 512, 512, 512, 2048, 1024, 192, 256, 256, 512, 128


def setup_inputs():
    n = np.random.standard_normal
    idx = np.random.permutation(T)[:J]
    idx2 = np.random.permutation(F)[:R]
    idx3 = np.stack([np.random.permutation(J)[:O] for _ in range(8)])
    idx4 = np.stack([np.random.permutation(C)[:O] for _ in range(8)])
    idx5 = np.stack([np.random.permutation(J)[:C] for _ in range(8)])
    idx6 = np.stack([np.random.permutation(U)[:C] for _ in range(8)])
    idx7 = np.stack([np.random.permutation(U)[:C] for _ in range(8)])
    fk = mx_kscale(K)
    fr = mx_kscale(R)
    tr = np.ones(F)
    tr[idx2] = fr
    xtp = pack_weight(n((K, T)) * fk[:, None], "e4m3")
    wtp = pack_weight(n((K, F)) * 1 / np.sqrt(K) / fk[:, None] * tr, "e4m3")
    wbp = pack_weight(n((R, N)) * 1 / np.sqrt(R) / fr[:, None], "e2m1")
    wop = pack_weight(n((R, N)) * 1 / np.sqrt(R) / fr[:, None], "e4m3")
    return {
        "xt_words": xtp[0],
        "xt_scales": xtp[1],
        "wt_words": wtp[0],
        "wt_scales": wtp[1],
        "sa": (np.random.uniform(0.5, 1.6, (R, 1))).astype(np.float32),
        "sb": (np.random.uniform(0.5, 1.6, (R, 1))).astype(np.float32),
        "wb_words": wbp[0],
        "wb_scales": wbp[1],
        "wo_words": wop[0],
        "wo_scales": wop[1],
        "offs": striped(idx),
        "offs2": striped(idx2),
        "offs3": striped8(idx3),
        "offs4": striped8(idx4),
        "offs5": striped8(idx5),
        "offs6": striped8(idx6),
        "offs7": striped8(idx7),
    }


def reference(xt_words, xt_scales, wt_words, wt_scales, sa, sb, wb_words, wb_scales, wo_words, wo_scales, offs, offs2, offs3, offs4, offs5, offs6, offs7):
    idx = unstriped(offs)
    idx2 = unstriped(offs2)
    idx3 = unstriped8(offs3)
    idx4 = unstriped8(offs4)
    idx5 = unstriped8(offs5)
    idx6 = unstriped8(offs6)
    idx7 = unstriped8(offs7)
    xtu = unpack_weight(xt_words, xt_scales, "e4m3")
    wtu = unpack_weight(wt_words, wt_scales, "e4m3")
    wbu = unpack_weight(wb_words, wb_scales, "e2m1")
    wou = unpack_weight(wo_words, wo_scales, "e4m3")
    wtidx2g = wtu[:, idx2]
    xtidxg = xtu[:, idx]
    a = wtidx2g.T @ xtidxg
    h1 = pick8(a, idx3, 64) * f64(sa)
    pw = np.zeros((R, C))
    pw[np.arange(R)[:, None], idx4[np.arange(R) % 512 // 64]] = h1
    hid = np.abs(pw - pick8(a, idx5, 64) * f64(sb))
    hidq = mxq(hid, 0, "e4m3")
    p = wbu.T @ hidq
    q = wou.T @ hidq
    m0 = np.zeros((N, U))
    m0[np.arange(N)[:, None], idx6[np.arange(N) % 128 // 16]] = p
    m1 = np.zeros((N, U))
    m1[np.arange(N)[:, None], idx7[np.arange(N) % 128 // 16]] = q
    m2 = m0.reshape(N, E, U // E).max(axis=2)
    m3 = m1.reshape(N, E, U // E).max(axis=2)
    y = m2 - m3
    return y

@@ -1,0 +1,237 @@
+from contextlib import ExitStack
+
+import concourse.mybir as mybir
+
+K, J, R, T, F, O, C, N, U, E = 512, 512, 512, 2048, 1024, 192, 256, 256, 512, 128
+FLOPS = 2 * K * R * J + 2 * 2 * R * N * C
+
+F32 = mybir.dt.float32
+BF16 = mybir.dt.bfloat16
+I32 = mybir.dt.int32
+U32 = mybir.dt.uint32
+U16 = mybir.dt.uint16
+U8 = mybir.dt.uint8
+FP8X4 = mybir.dt.float8_e4m3fn_x4
+FP4X4 = mybir.dt.float4_e2m1fn_x4
+ALU = mybir.AluOpType
+COPY = mybir.ActivationFunctionType.Copy
+
+P = 128
+PACK = 4
+HALF = C // 2
+W_ROW = 4
+SLOT_PIECES = ((0, 256), (256, 512))
+
+
+def load_scales(queue, plane, scales, first_row, quadrants=range(4)):
+    for q in quadrants:
+        row = 32 * q + first_row
+        queue.dma_start(out=plane[row : row + 4, :].bitcast(I32), in_=scales[0, 4 * q : 4 * q + 4, :].bitcast(I32))
+
+
+def tile_picked_tokens_store_one_wholepage_outcomes_endgap_kernel(
+    tc, xt_words, xt_scales, wt_words, wt_scales, sa, sb, wb_words, wb_scales, wo_words, wo_scales,
+    offs, offs2, offs3, offs4, offs5, offs6, offs7, out,
+):
+    nc = tc.nc
+    with ExitStack() as ctx:
+        lists = ctx.enter_context(tc.tile_pool(name="lists", bufs=1))
+        keep = ctx.enter_context(tc.tile_pool(name="keep", bufs=1))
+        psum = ctx.enter_context(tc.psum_pool(name="psum", bufs=1))
+
+        def load_list(src, name):
+            tile = lists.tile([P, src.shape[1]], U16, name=name)
+            nc.sync.dma_start(tile[:], src)
+            return tile
+
+        def zeroed_plane(width, name):
+            plane = keep.tile([P, width], U8, name=name, align_bytes=64)
+            nc.vector.memset(plane[:].bitcast(I32), 0)
+            return plane
+
+        wt_plane = zeroed_plane(F, "wt_plane")
+        xt_plane = zeroed_plane(T, "xt_plane")
+        wt_codes = keep.tile([P, F], U32, align_bytes=64)
+        nc.sync.dma_start(out=wt_codes[:].bitcast(I32), in_=wt_words[0].rearrange("p n t -> p (n t)").bitcast(I32))
+        load_scales(nc.scalar, wt_plane, wt_scales, W_ROW, range(3))
+        load_scales(nc.sync, wt_plane, wt_scales, W_ROW, range(3, 4))
+        feature_list = load_list(offs2, "feature_list")
+        xt_codes = keep.tile([P, T], U32, align_bytes=64)
+        nc.sync.dma_start(out=xt_codes[:].bitcast(I32), in_=xt_words[0].rearrange("p n t -> p (n t)").bitcast(I32))
+        token_list = load_list(offs, "token_list")
+        load_scales(nc.scalar, xt_plane, xt_scales, 0)
+
+        fill_slots = load_list(offs3, "fill_slots")
+        sa_sb = keep.tile([P, PACK], F32)
+        nc.sync.dma_start(out=sa_sb[:], in_=sa.rearrange("(p t) o -> p (t o)", t=PACK))
+        page_slots = load_list(offs5, "page_slots")
+        sb_sb = keep.tile([P, PACK], F32)
+        nc.sync.dma_start(out=sb_sb[:], in_=sb.rearrange("(p t) o -> p (t o)", t=PACK))
+        fill_columns = load_list(offs4, "fill_columns")
+
+        wb_plane = zeroed_plane(N, "wb_plane")
+        wo_plane = zeroed_plane(N, "wo_plane")
+        wb_codes = keep.tile([P, 2 * N], U8, align_bytes=64)
+        nc.sync.dma_start(out=wb_codes[:].bitcast(I32), in_=wb_words[0].bitcast(I32))
+        wo_codes = keep.tile([P, N], U32, align_bytes=64)
+        nc.sync.dma_start(out=wo_codes[:].bitcast(I32), in_=wo_words[0].rearrange("p n t -> p (n t)").bitcast(I32))
+        load_scales(nc.sync, wb_plane, wb_scales, 0)
+        load_scales(nc.sync, wo_plane, wo_scales, 0)
+        outcome_lists = [load_list(offs6, "first_columns"), load_list(offs7, "second_columns")]
+
+        pages = []
+        for t in range(PACK):
+            page = keep.tile([P, C], F32, name="page%d" % t)
+            nc.vector.memset(page[:], 0.0)
+            pages.append(page)
+
+        w_code = keep.tile([P, PACK, P], U32, tag="operand_then_page1", align_bytes=64)
+        nc.vector.tensor_copy(w_code[:].rearrange("p t m -> p m t"), wt_codes[:].indirect(feature_list[:]))
+        w_scale = keep.tile([P, PACK, P], U8, tag="operand_then_page0", align_bytes=64)
+        nc.vector.tensor_copy(w_scale[:].rearrange("p t m -> p m t"), wt_plane[:].indirect(feature_list[:]))
+        x_code = keep.tile([P, J], U32, tag="operand_then_page2", align_bytes=64)
+        nc.vector.tensor_copy(x_code[:], xt_codes[:].indirect(token_list[:]))
+        x_scale = []
+        for i, (lo, hi) in enumerate(SLOT_PIECES):
+            piece = keep.tile([P, hi - lo], U8, name="x_scale%d" % i, tag="operand_then_page%d" % (3 + i), align_bytes=64)
+            nc.vector.tensor_copy(piece[:], xt_plane[:].indirect(token_list[:, lo // 16 : hi // 16]))
+            x_scale.append(piece)
+
+        def first_product(t, i, acc):
+            lo, hi = SLOT_PIECES[i]
+            nc.tensor.matmul_mx(
+                out=acc,
+                lhsT=w_code[:, t, :].bitcast(FP8X4),
+                lhsT_scale=w_scale[W_ROW:P, t, :],
+                rhs=x_code[:, lo:hi].bitcast(FP8X4),
+                rhs_scale=x_scale[i][:],
+                start=True,
+                stop=True,
+            )
+
+        hidden = [keep.tile([P, J], F32, name="hidden%d" % t) for t in range(PACK)]
+        for i, (lo, hi) in enumerate(SLOT_PIECES):
+            acc = psum.tile([P, hi - lo], F32, name="acc0_%d" % i, tag="bank%d" % i)
+            first_product(0, i, acc[:])
+            nc.scalar.activation(hidden[0][:, lo:hi], acc[:], COPY)
+        for t in range(1, PACK):
+            acc = psum.tile([P, J], F32, name="acc%d" % t, tag="bank%d" % ((t - 1) % 2))
+            for i, (lo, hi) in enumerate(SLOT_PIECES):
+                first_product(t, i, acc[:, lo:hi])
+            nc.vector.tensor_copy(hidden[t][:], acc[:])
+
+        outcome_pages = []
+        for i in range(4):
+            page = keep.tile([P, U], F32, name="outcome_page%d" % i, tag="operand_then_page%d" % i, align_bytes=64)
+            nc.gpsimd.memset(page[:], 0.0)
+            outcome_pages.append(page)
+
+        fetched = [keep.tile([P, PACK, HALF], F32, name="fetched0")]
+        diff = [keep.tile([P, PACK, HALF], F32, name="diff0")]
+        hid = [keep.tile([P, HALF, PACK], BF16, name="hid0", tag="hid0", align_bytes=64)]
+
+        def fetch_page_half(t, h):
+            cols = slice(h * HALF // 16, (h + 1) * HALF // 16)
+            nc.scalar.activation(
+                fetched[h][:, t, :], hidden[t][:].indirect(page_slots[:, cols]), COPY, scale=sb_sb[:, t : t + 1]
+            )
+
+        def subtract(t, h):
+            nc.vector.tensor_tensor(
+                diff[h][:, t, :], pages[t][:, h * HALF : (h + 1) * HALF], fetched[h][:, t, :], ALU.subtract
+            )
+
+        for t in range(PACK):
+            filling = keep.tile([P, O], F32, name="filling%d" % t, tag="filling%d" % t)
+            nc.scalar.activation(filling[:], hidden[t][:].indirect(fill_slots[:]), COPY, scale=sa_sb[:, t : t + 1])
+            fetch_page_half(t, 0)
+            nc.scalar.activation(pages[t][:].indirect(fill_columns[:]), filling[:], COPY)
+            subtract(t, 0)
+            nc.vector.scalar_tensor_tensor(
+                hid[0][:, :, t], diff[0][:, t, :], -1.0, diff[0][:, t, :], ALU.mult, ALU.max
+            )
+
+        def quantise(h):
+            codes = keep.tile([P, HALF], U32, name="hid_code%d" % h, tag="hid_code%d" % h, align_bytes=64)
+            plane = keep.tile([P, HALF], U8, name="hid_plane%d" % h, align_bytes=64)
+            nc.vector.quantize_mx(
+                out=codes[:].bitcast(FP8X4), scales=plane[:], in_=hid[h][:].rearrange("p c t -> p (c t)")
+            )
+            return codes, plane
+
+        def second_product(i, acc, codes, plane):
+            cols = slice(i // 2 * P, (i // 2 + 1) * P)
+            if i % 2 == 0:
+                weights = wb_codes[:, 2 * cols.start : 2 * cols.stop].bitcast(FP4X4)
+                weight_plane = wb_plane
+            else:
+                weights = wo_codes[:, cols].bitcast(FP8X4)
+                weight_plane = wo_plane
+            nc.tensor.matmul_mx(
+                out=acc,
+                lhsT=weights,
+                lhsT_scale=weight_plane[:, cols],
+                rhs=codes[:].bitcast(FP8X4),
+                rhs_scale=plane[:],
+                start=True,
+                stop=True,
+            )
+
+        def put_outcome(i, h, values):
+            cols = slice(h * HALF // 16, (h + 1) * HALF // 16)
+            nc.scalar.activation(outcome_pages[i][:].indirect(outcome_lists[i % 2][:, cols]), values, COPY)
+
+        codes, plane = quantise(0)
+        outcomes = [[], []]
+        early = []
+        for i in range(2):
+            acc = psum.tile([P, HALF], F32, name="early%d" % i, tag="bank%d" % (3 + i))
+            second_product(i, acc[:], codes, plane)
+            early.append(acc)
+        acc_rest = psum.tile([P, 2, HALF], F32, tag="bank2")
+        for i in range(2, 4):
+            second_product(i, acc_rest[:, i - 2, :], codes, plane)
+        early_rest = keep.tile([P, 2, HALF], F32)
+        nc.vector.tensor_copy(early_rest[:], acc_rest[:])
+
+        diff.append(keep.tile([P, PACK, HALF], F32, name="diff1", tag="hid0", align_bytes=64))
+        fetched.append(keep.tile([P, PACK, HALF], F32, name="fetched1", tag="filling3"))
+        for t in range(PACK):
+            fetch_page_half(t, 1)
+            subtract(t, 1)
+        hid.append(keep.tile([P, HALF, PACK], BF16, name="hid1", tag="hid_code0", align_bytes=64))
+        magnitude = keep.tile([P, PACK, HALF], BF16)
+        nc.vector.scalar_tensor_tensor(magnitude[:], diff[1][:], -1.0, diff[1][:], ALU.mult, ALU.max)
+        nc.vector.tensor_copy(
+            hid[1][:].rearrange("p (c i) t -> p c t i", i=4), magnitude[:].rearrange("p t (c i) -> p c t i", i=4)
+        )
+        codes, plane = quantise(1)
+        acc_first = psum.tile([P, HALF], F32, tag="bank2")
+        second_product(0, acc_first[:], codes, plane)
+        late_first = keep.tile([P, HALF], F32)
+        nc.vector.tensor_copy(late_first[:], acc_first[:])
+        acc_second = psum.tile([P, 3, HALF], F32, tag="bank7")
+        for i in range(1, 4):
+            second_product(i, acc_second[:, i - 1, :], codes, plane)
+        late_rest = keep.tile([P, 3, HALF], F32)
+        nc.vector.tensor_copy(late_rest[:], acc_second[:])
+        outcomes[1] = [late_first[:]] + [late_rest[:, i, :] for i in range(3)]
+
+        for i in range(2):
+            values = keep.tile([P, HALF], F32, name="early_values%d" % i)
+            nc.scalar.copy(values[:], early[i][:])
+            outcomes[0].append(values[:])
+        outcomes[0].extend([early_rest[:, i, :] for i in range(2)])
+        for i in range(4):
+            put_outcome(i, 0, outcomes[0][i])
+        largest = keep.tile([P, 4, E], F32)
+        for i in range(4):
+            put_outcome(i, 1, outcomes[1][i])
+            nc.vector.tensor_reduce(
+                largest[:, i, :], outcome_pages[i][:].rearrange("p (e u) -> p e u", u=U // E),
+                mybir.AxisListType.X, ALU.max,
+            )
+            if i % 2 == 1:
+                gap = keep.tile([P, E], F32, name="gap%d" % (i // 2))
+                nc.vector.tensor_tensor(gap[:], largest[:, i - 1, :], largest[:, i, :], ALU.subtract)
+                nc.sync.dma_start(out=out[i // 2 * P : (i // 2 + 1) * P, :], in_=gap[:])

@@ -23,12 +23,6 @@ W_ROW = 4
 SLOT_PIECES = ((0, 256), (256, 512))
 
 
-def load_scales(queue, plane, scales, first_row, quadrants=range(4)):
-    for q in quadrants:
-        row = 32 * q + first_row
-        queue.dma_start(out=plane[row : row + 4, :].bitcast(I32), in_=scales[0, 4 * q : 4 * q + 4, :].bitcast(I32))
-
-
 def tile_picked_tokens_store_one_wholepage_outcomes_endgap_kernel(
     tc, xt_words, xt_scales, wt_words, wt_scales, sa, sb, wb_words, wb_scales, wo_words, wo_scales,
     offs, offs2, offs3, offs4, offs5, offs6, offs7, out,
@@ -49,25 +43,30 @@ def tile_picked_tokens_store_one_wholepage_outcomes_endgap_kernel(
             nc.vector.memset(plane[:].bitcast(I32), 0)
             return plane
 
+        def load_scales(plane, scales, first_row):
+            for q in range(4):
+                row = 32 * q + first_row
+                nc.sync.dma_start(
+                    out=plane[row : row + 4, :].bitcast(I32), in_=scales[0, 4 * q : 4 * q + 4, :].bitcast(I32)
+                )
+
         wt_plane = zeroed_plane(F, "wt_plane")
         xt_plane = zeroed_plane(T, "xt_plane")
         wt_codes = keep.tile([P, F], U32, align_bytes=64)
         nc.sync.dma_start(out=wt_codes[:].bitcast(I32), in_=wt_words[0].rearrange("p n t -> p (n t)").bitcast(I32))
-        load_scales(nc.scalar, wt_plane, wt_scales, W_ROW, range(3))
-        load_scales(nc.sync, wt_plane, wt_scales, W_ROW, range(3, 4))
         feature_list = load_list(offs2, "feature_list")
+        load_scales(wt_plane, wt_scales, W_ROW)
+        token_list = load_list(offs, "token_list")
         xt_codes = keep.tile([P, T], U32, align_bytes=64)
         nc.sync.dma_start(out=xt_codes[:].bitcast(I32), in_=xt_words[0].rearrange("p n t -> p (n t)").bitcast(I32))
-        token_list = load_list(offs, "token_list")
-        load_scales(nc.scalar, xt_plane, xt_scales, 0)
-
         fill_slots = load_list(offs3, "fill_slots")
+        page_slots = load_list(offs5, "page_slots")
+        fill_columns = load_list(offs4, "fill_columns")
+        load_scales(xt_plane, xt_scales, 0)
         sa_sb = keep.tile([P, PACK], F32)
         nc.sync.dma_start(out=sa_sb[:], in_=sa.rearrange("(p t) o -> p (t o)", t=PACK))
-        page_slots = load_list(offs5, "page_slots")
         sb_sb = keep.tile([P, PACK], F32)
         nc.sync.dma_start(out=sb_sb[:], in_=sb.rearrange("(p t) o -> p (t o)", t=PACK))
-        fill_columns = load_list(offs4, "fill_columns")
 
         wb_plane = zeroed_plane(N, "wb_plane")
         wo_plane = zeroed_plane(N, "wo_plane")
@@ -75,8 +74,8 @@ def tile_picked_tokens_store_one_wholepage_outcomes_endgap_kernel(
         nc.sync.dma_start(out=wb_codes[:].bitcast(I32), in_=wb_words[0].bitcast(I32))
         wo_codes = keep.tile([P, N], U32, align_bytes=64)
         nc.sync.dma_start(out=wo_codes[:].bitcast(I32), in_=wo_words[0].rearrange("p n t -> p (n t)").bitcast(I32))
-        load_scales(nc.sync, wb_plane, wb_scales, 0)
-        load_scales(nc.sync, wo_plane, wo_scales, 0)
+        load_scales(wb_plane, wb_scales, 0)
+        load_scales(wo_plane, wo_scales, 0)
         outcome_lists = [load_list(offs6, "first_columns"), load_list(offs7, "second_columns")]
 
         pages = []
@@ -123,7 +122,7 @@ def tile_picked_tokens_store_one_wholepage_outcomes_endgap_kernel(
         outcome_pages = []
         for i in range(4):
             page = keep.tile([P, U], F32, name="outcome_page%d" % i, tag="operand_then_page%d" % i, align_bytes=64)
-            nc.gpsimd.memset(page[:], 0.0)
+            nc.vector.memset(page[:], 0.0)
             outcome_pages.append(page)
 
         fetched = [keep.tile([P, PACK, HALF], F32, name="fetched0")]

@@ -19,8 +19,9 @@ COPY = mybir.ActivationFunctionType.Copy
 P = 128
 PACK = 4
 HALF = C // 2
+QUARTER = C // 4
 W_ROW = 4
-SLOT_PIECES = ((0, 256), (256, 512))
+SLOT_PIECES = ((0, 256), (256, 384), (384, 512))
 
 
 def tile_picked_tokens_store_one_wholepage_outcomes_endgap_kernel(
@@ -52,21 +53,21 @@ def tile_picked_tokens_store_one_wholepage_outcomes_endgap_kernel(
 
         wt_plane = zeroed_plane(F, "wt_plane")
         xt_plane = zeroed_plane(T, "xt_plane")
-        wt_codes = keep.tile([P, F], U32, align_bytes=64)
-        nc.sync.dma_start(out=wt_codes[:].bitcast(I32), in_=wt_words[0].rearrange("p n t -> p (n t)").bitcast(I32))
         feature_list = load_list(offs2, "feature_list")
         load_scales(wt_plane, wt_scales, W_ROW)
+        wt_codes = keep.tile([P, F], U32, align_bytes=64)
+        nc.sync.dma_start(out=wt_codes[:].bitcast(I32), in_=wt_words[0].rearrange("p n t -> p (n t)").bitcast(I32))
         token_list = load_list(offs, "token_list")
+        load_scales(xt_plane, xt_scales, 0)
         xt_codes = keep.tile([P, T], U32, align_bytes=64)
         nc.sync.dma_start(out=xt_codes[:].bitcast(I32), in_=xt_words[0].rearrange("p n t -> p (n t)").bitcast(I32))
-        fill_slots = load_list(offs3, "fill_slots")
-        page_slots = load_list(offs5, "page_slots")
-        fill_columns = load_list(offs4, "fill_columns")
-        load_scales(xt_plane, xt_scales, 0)
         sa_sb = keep.tile([P, PACK], F32)
         nc.sync.dma_start(out=sa_sb[:], in_=sa.rearrange("(p t) o -> p (t o)", t=PACK))
+        fill_slots = load_list(offs3, "fill_slots")
         sb_sb = keep.tile([P, PACK], F32)
         nc.sync.dma_start(out=sb_sb[:], in_=sb.rearrange("(p t) o -> p (t o)", t=PACK))
+        page_slots = load_list(offs5, "page_slots")
+        fill_columns = load_list(offs4, "fill_columns")
 
         wb_plane = zeroed_plane(N, "wb_plane")
         wo_plane = zeroed_plane(N, "wo_plane")
@@ -84,17 +85,17 @@ def tile_picked_tokens_store_one_wholepage_outcomes_endgap_kernel(
             nc.vector.memset(page[:], 0.0)
             pages.append(page)
 
-        w_code = keep.tile([P, PACK, P], U32, tag="operand_then_page1", align_bytes=64)
-        nc.vector.tensor_copy(w_code[:].rearrange("p t m -> p m t"), wt_codes[:].indirect(feature_list[:]))
         w_scale = keep.tile([P, PACK, P], U8, tag="operand_then_page0", align_bytes=64)
         nc.vector.tensor_copy(w_scale[:].rearrange("p t m -> p m t"), wt_plane[:].indirect(feature_list[:]))
-        x_code = keep.tile([P, J], U32, tag="operand_then_page2", align_bytes=64)
-        nc.vector.tensor_copy(x_code[:], xt_codes[:].indirect(token_list[:]))
-        x_scale = []
+        w_code = keep.tile([P, PACK, P], U32, tag="operand_then_page1", align_bytes=64)
+        nc.vector.tensor_copy(w_code[:].rearrange("p t m -> p m t"), wt_codes[:].indirect(feature_list[:]))
+        x_scale = keep.tile([P, J], U8, tag="operand_then_page2", align_bytes=64)
+        nc.vector.tensor_copy(x_scale[:], xt_plane[:].indirect(token_list[:]))
+        x_code = []
         for i, (lo, hi) in enumerate(SLOT_PIECES):
-            piece = keep.tile([P, hi - lo], U8, name="x_scale%d" % i, tag="operand_then_page%d" % (3 + i), align_bytes=64)
-            nc.vector.tensor_copy(piece[:], xt_plane[:].indirect(token_list[:, lo // 16 : hi // 16]))
-            x_scale.append(piece)
+            piece = keep.tile([P, hi - lo], U32, name="x_code%d" % i, tag="operand_then_page%d" % (3 + i), align_bytes=64)
+            nc.vector.tensor_copy(piece[:], xt_codes[:].indirect(token_list[:, lo // 16 : hi // 16]))
+            x_code.append(piece)
 
         def first_product(t, i, acc):
             lo, hi = SLOT_PIECES[i]
@@ -102,8 +103,8 @@ def tile_picked_tokens_store_one_wholepage_outcomes_endgap_kernel(
                 out=acc,
                 lhsT=w_code[:, t, :].bitcast(FP8X4),
                 lhsT_scale=w_scale[W_ROW:P, t, :],
-                rhs=x_code[:, lo:hi].bitcast(FP8X4),
-                rhs_scale=x_scale[i][:],
+                rhs=x_code[i][:].bitcast(FP8X4),
+                rhs_scale=x_scale[:, lo:hi],
                 start=True,
                 stop=True,
             )
@@ -114,7 +115,7 @@ def tile_picked_tokens_store_one_wholepage_outcomes_endgap_kernel(
             first_product(0, i, acc[:])
             nc.scalar.activation(hidden[0][:, lo:hi], acc[:], COPY)
         for t in range(1, PACK):
-            acc = psum.tile([P, J], F32, name="acc%d" % t, tag="bank%d" % ((t - 1) % 2))
+            acc = psum.tile([P, J], F32, name="acc%d" % t, tag="bank%d" % (t % 3))
             for i, (lo, hi) in enumerate(SLOT_PIECES):
                 first_product(t, i, acc[:, lo:hi])
             nc.vector.tensor_copy(hidden[t][:], acc[:])
@@ -127,7 +128,10 @@ def tile_picked_tokens_store_one_wholepage_outcomes_endgap_kernel(
 
         fetched = [keep.tile([P, PACK, HALF], F32, name="fetched0")]
         diff = [keep.tile([P, PACK, HALF], F32, name="diff0")]
-        hid = [keep.tile([P, HALF, PACK], BF16, name="hid0", tag="hid0", align_bytes=64)]
+        hid_quarter = [
+            keep.tile([P, QUARTER, PACK], BF16, name="hid_quarter%d" % s, tag="hid_quarter%d" % s, align_bytes=64)
+            for s in range(2)
+        ]
 
         def fetch_page_half(t, h):
             cols = slice(h * HALF // 16, (h + 1) * HALF // 16)
@@ -135,9 +139,9 @@ def tile_picked_tokens_store_one_wholepage_outcomes_endgap_kernel(
                 fetched[h][:, t, :], hidden[t][:].indirect(page_slots[:, cols]), COPY, scale=sb_sb[:, t : t + 1]
             )
 
-        def subtract(t, h):
+        def subtract(t, h, lo, hi):
             nc.vector.tensor_tensor(
-                diff[h][:, t, :], pages[t][:, h * HALF : (h + 1) * HALF], fetched[h][:, t, :], ALU.subtract
+                diff[h][:, t, lo:hi], pages[t][:, h * HALF + lo : h * HALF + hi], fetched[h][:, t, lo:hi], ALU.subtract
             )
 
         for t in range(PACK):
@@ -145,18 +149,14 @@ def tile_picked_tokens_store_one_wholepage_outcomes_endgap_kernel(
             nc.scalar.activation(filling[:], hidden[t][:].indirect(fill_slots[:]), COPY, scale=sa_sb[:, t : t + 1])
             fetch_page_half(t, 0)
             nc.scalar.activation(pages[t][:].indirect(fill_columns[:]), filling[:], COPY)
-            subtract(t, 0)
-            nc.vector.scalar_tensor_tensor(
-                hid[0][:, :, t], diff[0][:, t, :], -1.0, diff[0][:, t, :], ALU.mult, ALU.max
-            )
+            for s in range(2):
+                subtract(t, 0, s * QUARTER, (s + 1) * QUARTER)
+            for s in range(2):
+                part = diff[0][:, t, s * QUARTER : (s + 1) * QUARTER]
+                nc.vector.scalar_tensor_tensor(hid_quarter[s][:, :, t], part, -1.0, part, ALU.mult, ALU.max)
 
-        def quantise(h):
-            codes = keep.tile([P, HALF], U32, name="hid_code%d" % h, tag="hid_code%d" % h, align_bytes=64)
-            plane = keep.tile([P, HALF], U8, name="hid_plane%d" % h, align_bytes=64)
-            nc.vector.quantize_mx(
-                out=codes[:].bitcast(FP8X4), scales=plane[:], in_=hid[h][:].rearrange("p c t -> p (c t)")
-            )
-            return codes, plane
+        def quantise(values, codes, plane):
+            nc.vector.quantize_mx(out=codes.bitcast(FP8X4), scales=plane, in_=values[:].rearrange("p c t -> p (c t)"))
 
         def second_product(i, acc, codes, plane):
             cols = slice(i // 2 * P, (i // 2 + 1) * P)
@@ -170,62 +170,72 @@ def tile_picked_tokens_store_one_wholepage_outcomes_endgap_kernel(
                 out=acc,
                 lhsT=weights,
                 lhsT_scale=weight_plane[:, cols],
-                rhs=codes[:].bitcast(FP8X4),
-                rhs_scale=plane[:],
+                rhs=codes.bitcast(FP8X4),
+                rhs_scale=plane,
                 start=True,
                 stop=True,
             )
 
-        def put_outcome(i, h, values):
-            cols = slice(h * HALF // 16, (h + 1) * HALF // 16)
-            nc.scalar.activation(outcome_pages[i][:].indirect(outcome_lists[i % 2][:, cols]), values, COPY)
+        def put_outcome(i, lo, hi, values):
+            nc.scalar.activation(outcome_pages[i][:].indirect(outcome_lists[i % 2][:, lo // 16 : hi // 16]), values, COPY)
 
-        codes, plane = quantise(0)
-        outcomes = [[], []]
+        codes = keep.tile([P, HALF], U32, name="codes_first", tag="codes_first", align_bytes=64)
+        plane = keep.tile([P, HALF], U8, name="plane_first", align_bytes=64)
+        quarters = [slice(s * QUARTER, (s + 1) * QUARTER) for s in range(2)]
+        for s in range(2):
+            quantise(hid_quarter[s], codes[:, quarters[s]], plane[:, quarters[s]])
         early = []
-        for i in range(2):
-            acc = psum.tile([P, HALF], F32, name="early%d" % i, tag="bank%d" % (3 + i))
-            second_product(i, acc[:], codes, plane)
+        for j in range(2):
+            acc = psum.tile([P, QUARTER], F32, name="early%d" % j, tag="bank%d" % (3 + j))
+            second_product(2 * j + 1, acc[:], codes[:, quarters[0]], plane[:, quarters[0]])
             early.append(acc)
-        acc_rest = psum.tile([P, 2, HALF], F32, tag="bank2")
-        for i in range(2, 4):
-            second_product(i, acc_rest[:, i - 2, :], codes, plane)
-        early_rest = keep.tile([P, 2, HALF], F32)
-        nc.vector.tensor_copy(early_rest[:], acc_rest[:])
+        acc_q = psum.tile([P, 2, QUARTER], F32, tag="bank0")
+        for j in range(2):
+            second_product(2 * j + 1, acc_q[:, j, :], codes[:, quarters[1]], plane[:, quarters[1]])
+        q_second = keep.tile([P, 2, QUARTER], F32)
+        nc.vector.tensor_copy(q_second[:], acc_q[:])
+        acc_p = psum.tile([P, 2, HALF], F32, tag="bank5")
+        for j in range(2):
+            second_product(2 * j, acc_p[:, j, :], codes[:], plane[:])
+        p_first = keep.tile([P, 2, HALF], F32)
+        nc.vector.tensor_copy(p_first[:], acc_p[:])
 
-        diff.append(keep.tile([P, PACK, HALF], F32, name="diff1", tag="hid0", align_bytes=64))
+        diff.append(keep.tile([P, PACK, HALF], F32, name="diff1", tag="hid_quarter1", align_bytes=64))
         fetched.append(keep.tile([P, PACK, HALF], F32, name="fetched1", tag="filling3"))
         for t in range(PACK):
             fetch_page_half(t, 1)
-            subtract(t, 1)
-        hid.append(keep.tile([P, HALF, PACK], BF16, name="hid1", tag="hid_code0", align_bytes=64))
-        magnitude = keep.tile([P, PACK, HALF], BF16)
-        nc.vector.scalar_tensor_tensor(magnitude[:], diff[1][:], -1.0, diff[1][:], ALU.mult, ALU.max)
-        nc.vector.tensor_copy(
-            hid[1][:].rearrange("p (c i) t -> p c t i", i=4), magnitude[:].rearrange("p t (c i) -> p c t i", i=4)
-        )
-        codes, plane = quantise(1)
-        acc_first = psum.tile([P, HALF], F32, tag="bank2")
-        second_product(0, acc_first[:], codes, plane)
+            subtract(t, 1, 0, HALF)
+        hid_late = keep.tile([P, HALF, PACK], BF16, tag="codes_first", align_bytes=64)
+        by_column = diff[1][:].rearrange("p t c -> p c t")
+        nc.vector.scalar_tensor_tensor(hid_late[:], by_column, -1.0, by_column, ALU.mult, ALU.max)
+        codes_late = keep.tile([P, HALF], U32, align_bytes=64)
+        plane_late = keep.tile([P, HALF], U8, align_bytes=64)
+        quantise(hid_late, codes_late[:], plane_late[:])
+        acc_first = psum.tile([P, HALF], F32, tag="bank6")
+        second_product(0, acc_first[:], codes_late[:], plane_late[:])
         late_first = keep.tile([P, HALF], F32)
         nc.vector.tensor_copy(late_first[:], acc_first[:])
         acc_second = psum.tile([P, 3, HALF], F32, tag="bank7")
         for i in range(1, 4):
-            second_product(i, acc_second[:, i - 1, :], codes, plane)
+            second_product(i, acc_second[:, i - 1, :], codes_late[:], plane_late[:])
         late_rest = keep.tile([P, 3, HALF], F32)
         nc.vector.tensor_copy(late_rest[:], acc_second[:])
-        outcomes[1] = [late_first[:]] + [late_rest[:, i, :] for i in range(3)]
+        late = [late_first[:]] + [late_rest[:, i, :] for i in range(3)]
 
-        for i in range(2):
-            values = keep.tile([P, HALF], F32, name="early_values%d" % i)
-            nc.scalar.copy(values[:], early[i][:])
-            outcomes[0].append(values[:])
-        outcomes[0].extend([early_rest[:, i, :] for i in range(2)])
-        for i in range(4):
-            put_outcome(i, 0, outcomes[0][i])
+        q_first = []
+        for j in range(2):
+            values = keep.tile([P, QUARTER], F32, name="q_first%d" % j)
+            nc.scalar.copy(values[:], early[j][:])
+            q_first.append(values)
+        for j in range(2):
+            put_outcome(2 * j + 1, 0, QUARTER, q_first[j][:])
+        for j in range(2):
+            put_outcome(2 * j + 1, QUARTER, HALF, q_second[:, j, :])
+        for j in range(2):
+            put_outcome(2 * j, 0, HALF, p_first[:, j, :])
         largest = keep.tile([P, 4, E], F32)
         for i in range(4):
-            put_outcome(i, 1, outcomes[1][i])
+            put_outcome(i, HALF, C, late[i])
             nc.vector.tensor_reduce(
                 largest[:, i, :], outcome_pages[i][:].rearrange("p (e u) -> p e u", u=U // E),
                 mybir.AxisListType.X, ALU.max,

from contextlib import ExitStack

import concourse.mybir as mybir

K, J, R, T, F, O, C, N, U, E = 512, 512, 512, 2048, 1024, 192, 256, 256, 512, 128
FLOPS = 2 * K * R * J + 2 * 2 * R * N * C

F32 = mybir.dt.float32
BF16 = mybir.dt.bfloat16
I32 = mybir.dt.int32
U32 = mybir.dt.uint32
U16 = mybir.dt.uint16
U8 = mybir.dt.uint8
FP8X4 = mybir.dt.float8_e4m3fn_x4
FP4X4 = mybir.dt.float4_e2m1fn_x4
ALU = mybir.AluOpType
COPY = mybir.ActivationFunctionType.Copy

P = 128
PACK = 4
HALF = C // 2
QUARTER = C // 4
W_ROW = 4
SLOT_PIECES = ((0, 256), (256, 384), (384, 512))


def tile_picked_tokens_store_one_wholepage_outcomes_endgap_kernel(
    tc, xt_words, xt_scales, wt_words, wt_scales, sa, sb, wb_words, wb_scales, wo_words, wo_scales,
    offs, offs2, offs3, offs4, offs5, offs6, offs7, out,
):
    nc = tc.nc
    with ExitStack() as ctx:
        lists = ctx.enter_context(tc.tile_pool(name="lists", bufs=1))
        keep = ctx.enter_context(tc.tile_pool(name="keep", bufs=1))
        psum = ctx.enter_context(tc.psum_pool(name="psum", bufs=1))

        def load_list(src, name):
            tile = lists.tile([P, src.shape[1]], U16, name=name)
            nc.sync.dma_start(tile[:], src)
            return tile

        def zeroed_plane(width, name):
            plane = keep.tile([P, width], U8, name=name, align_bytes=64)
            nc.vector.memset(plane[:].bitcast(I32), 0)
            return plane

        def load_scales(plane, scales, first_row):
            for q in range(4):
                row = 32 * q + first_row
                nc.sync.dma_start(
                    out=plane[row : row + 4, :].bitcast(I32), in_=scales[0, 4 * q : 4 * q + 4, :].bitcast(I32)
                )

        wt_plane = zeroed_plane(F, "wt_plane")
        xt_plane = zeroed_plane(T, "xt_plane")
        feature_list = load_list(offs2, "feature_list")
        load_scales(wt_plane, wt_scales, W_ROW)
        wt_codes = keep.tile([P, F], U32, align_bytes=64)
        nc.sync.dma_start(out=wt_codes[:].bitcast(I32), in_=wt_words[0].rearrange("p n t -> p (n t)").bitcast(I32))
        token_list = load_list(offs, "token_list")
        load_scales(xt_plane, xt_scales, 0)
        xt_codes = keep.tile([P, T], U32, align_bytes=64)
        nc.sync.dma_start(out=xt_codes[:].bitcast(I32), in_=xt_words[0].rearrange("p n t -> p (n t)").bitcast(I32))
        sa_sb = keep.tile([P, PACK], F32)
        nc.sync.dma_start(out=sa_sb[:], in_=sa.rearrange("(p t) o -> p (t o)", t=PACK))
        fill_slots = load_list(offs3, "fill_slots")
        sb_sb = keep.tile([P, PACK], F32)
        nc.sync.dma_start(out=sb_sb[:], in_=sb.rearrange("(p t) o -> p (t o)", t=PACK))
        page_slots = load_list(offs5, "page_slots")
        fill_columns = load_list(offs4, "fill_columns")

        wb_plane = zeroed_plane(N, "wb_plane")
        wo_plane = zeroed_plane(N, "wo_plane")
        wb_codes = keep.tile([P, 2 * N], U8, align_bytes=64)
        nc.sync.dma_start(out=wb_codes[:].bitcast(I32), in_=wb_words[0].bitcast(I32))
        wo_codes = keep.tile([P, N], U32, align_bytes=64)
        nc.sync.dma_start(out=wo_codes[:].bitcast(I32), in_=wo_words[0].rearrange("p n t -> p (n t)").bitcast(I32))
        load_scales(wb_plane, wb_scales, 0)
        load_scales(wo_plane, wo_scales, 0)
        outcome_lists = [load_list(offs6, "first_columns"), load_list(offs7, "second_columns")]

        pages = []
        for t in range(PACK):
            page = keep.tile([P, C], F32, name="page%d" % t)
            nc.vector.memset(page[:], 0.0)
            pages.append(page)

        w_scale = keep.tile([P, PACK, P], U8, tag="operand_then_page0", align_bytes=64)
        nc.vector.tensor_copy(w_scale[:].rearrange("p t m -> p m t"), wt_plane[:].indirect(feature_list[:]))
        w_code = keep.tile([P, PACK, P], U32, tag="operand_then_page1", align_bytes=64)
        nc.vector.tensor_copy(w_code[:].rearrange("p t m -> p m t"), wt_codes[:].indirect(feature_list[:]))
        x_scale = keep.tile([P, J], U8, tag="operand_then_page2", align_bytes=64)
        nc.vector.tensor_copy(x_scale[:], xt_plane[:].indirect(token_list[:]))
        x_code = []
        for i, (lo, hi) in enumerate(SLOT_PIECES):
            piece = keep.tile([P, hi - lo], U32, name="x_code%d" % i, tag="operand_then_page%d" % (3 + i), align_bytes=64)
            nc.vector.tensor_copy(piece[:], xt_codes[:].indirect(token_list[:, lo // 16 : hi // 16]))
            x_code.append(piece)

        def first_product(t, i, acc):
            lo, hi = SLOT_PIECES[i]
            nc.tensor.matmul_mx(
                out=acc,
                lhsT=w_code[:, t, :].bitcast(FP8X4),
                lhsT_scale=w_scale[W_ROW:P, t, :],
                rhs=x_code[i][:].bitcast(FP8X4),
                rhs_scale=x_scale[:, lo:hi],
                start=True,
                stop=True,
            )

        hidden = [keep.tile([P, J], F32, name="hidden%d" % t) for t in range(PACK)]
        for i, (lo, hi) in enumerate(SLOT_PIECES):
            acc = psum.tile([P, hi - lo], F32, name="acc0_%d" % i, tag="bank%d" % i)
            first_product(0, i, acc[:])
            nc.scalar.activation(hidden[0][:, lo:hi], acc[:], COPY)
        for t in range(1, PACK):
            acc = psum.tile([P, J], F32, name="acc%d" % t, tag="bank%d" % (t % 3))
            for i, (lo, hi) in enumerate(SLOT_PIECES):
                first_product(t, i, acc[:, lo:hi])
            nc.vector.tensor_copy(hidden[t][:], acc[:])

        outcome_pages = []
        for i in range(4):
            page = keep.tile([P, U], F32, name="outcome_page%d" % i, tag="operand_then_page%d" % i, align_bytes=64)
            nc.vector.memset(page[:], 0.0)
            outcome_pages.append(page)

        fetched = [keep.tile([P, PACK, HALF], F32, name="fetched0")]
        diff = [keep.tile([P, PACK, HALF], F32, name="diff0")]
        hid_quarter = [
            keep.tile([P, QUARTER, PACK], BF16, name="hid_quarter%d" % s, tag="hid_quarter%d" % s, align_bytes=64)
            for s in range(2)
        ]

        def fetch_page_half(t, h):
            cols = slice(h * HALF // 16, (h + 1) * HALF // 16)
            nc.scalar.activation(
                fetched[h][:, t, :], hidden[t][:].indirect(page_slots[:, cols]), COPY, scale=sb_sb[:, t : t + 1]
            )

        def subtract(t, h, lo, hi):
            nc.vector.tensor_tensor(
                diff[h][:, t, lo:hi], pages[t][:, h * HALF + lo : h * HALF + hi], fetched[h][:, t, lo:hi], ALU.subtract
            )

        for t in range(PACK):
            filling = keep.tile([P, O], F32, name="filling%d" % t, tag="filling%d" % t)
            nc.scalar.activation(filling[:], hidden[t][:].indirect(fill_slots[:]), COPY, scale=sa_sb[:, t : t + 1])
            fetch_page_half(t, 0)
            nc.scalar.activation(pages[t][:].indirect(fill_columns[:]), filling[:], COPY)
            for s in range(2):
                subtract(t, 0, s * QUARTER, (s + 1) * QUARTER)
            for s in range(2):
                part = diff[0][:, t, s * QUARTER : (s + 1) * QUARTER]
                nc.vector.scalar_tensor_tensor(hid_quarter[s][:, :, t], part, -1.0, part, ALU.mult, ALU.max)

        def quantise(values, codes, plane):
            nc.vector.quantize_mx(out=codes.bitcast(FP8X4), scales=plane, in_=values[:].rearrange("p c t -> p (c t)"))

        def second_product(i, acc, codes, plane):
            cols = slice(i // 2 * P, (i // 2 + 1) * P)
            if i % 2 == 0:
                weights = wb_codes[:, 2 * cols.start : 2 * cols.stop].bitcast(FP4X4)
                weight_plane = wb_plane
            else:
                weights = wo_codes[:, cols].bitcast(FP8X4)
                weight_plane = wo_plane
            nc.tensor.matmul_mx(
                out=acc,
                lhsT=weights,
                lhsT_scale=weight_plane[:, cols],
                rhs=codes.bitcast(FP8X4),
                rhs_scale=plane,
                start=True,
                stop=True,
            )

        def put_outcome(i, lo, hi, values):
            nc.scalar.activation(outcome_pages[i][:].indirect(outcome_lists[i % 2][:, lo // 16 : hi // 16]), values, COPY)

        codes = keep.tile([P, HALF], U32, name="codes_first", tag="codes_first", align_bytes=64)
        plane = keep.tile([P, HALF], U8, name="plane_first", align_bytes=64)
        quarters = [slice(s * QUARTER, (s + 1) * QUARTER) for s in range(2)]
        for s in range(2):
            quantise(hid_quarter[s], codes[:, quarters[s]], plane[:, quarters[s]])
        early = []
        for j in range(2):
            acc = psum.tile([P, QUARTER], F32, name="early%d" % j, tag="bank%d" % (3 + j))
            second_product(2 * j + 1, acc[:], codes[:, quarters[0]], plane[:, quarters[0]])
            early.append(acc)
        acc_q = psum.tile([P, 2, QUARTER], F32, tag="bank0")
        for j in range(2):
            second_product(2 * j + 1, acc_q[:, j, :], codes[:, quarters[1]], plane[:, quarters[1]])
        q_second = keep.tile([P, 2, QUARTER], F32)
        nc.vector.tensor_copy(q_second[:], acc_q[:])
        acc_p = psum.tile([P, 2, HALF], F32, tag="bank5")
        for j in range(2):
            second_product(2 * j, acc_p[:, j, :], codes[:], plane[:])
        p_first = keep.tile([P, 2, HALF], F32)
        nc.vector.tensor_copy(p_first[:], acc_p[:])

        diff.append(keep.tile([P, PACK, HALF], F32, name="diff1", tag="hid_quarter1", align_bytes=64))
        fetched.append(keep.tile([P, PACK, HALF], F32, name="fetched1", tag="filling3"))
        for t in range(PACK):
            fetch_page_half(t, 1)
            subtract(t, 1, 0, HALF)
        hid_late = keep.tile([P, HALF, PACK], BF16, tag="codes_first", align_bytes=64)
        by_column = diff[1][:].rearrange("p t c -> p c t")
        nc.vector.scalar_tensor_tensor(hid_late[:], by_column, -1.0, by_column, ALU.mult, ALU.max)
        codes_late = keep.tile([P, HALF], U32, align_bytes=64)
        plane_late = keep.tile([P, HALF], U8, align_bytes=64)
        quantise(hid_late, codes_late[:], plane_late[:])
        acc_first = psum.tile([P, HALF], F32, tag="bank6")
        second_product(0, acc_first[:], codes_late[:], plane_late[:])
        late_first = keep.tile([P, HALF], F32)
        nc.vector.tensor_copy(late_first[:], acc_first[:])
        acc_second = psum.tile([P, 3, HALF], F32, tag="bank7")
        for i in range(1, 4):
            second_product(i, acc_second[:, i - 1, :], codes_late[:], plane_late[:])
        late_rest = keep.tile([P, 3, HALF], F32)
        nc.vector.tensor_copy(late_rest[:], acc_second[:])
        late = [late_first[:]] + [late_rest[:, i, :] for i in range(3)]

        q_first = []
        for j in range(2):
            values = keep.tile([P, QUARTER], F32, name="q_first%d" % j)
            nc.scalar.copy(values[:], early[j][:])
            q_first.append(values)
        for j in range(2):
            put_outcome(2 * j + 1, 0, QUARTER, q_first[j][:])
        for j in range(2):
            put_outcome(2 * j + 1, QUARTER, HALF, q_second[:, j, :])
        for j in range(2):
            put_outcome(2 * j, 0, HALF, p_first[:, j, :])
        largest = keep.tile([P, 4, E], F32)
        for i in range(4):
            put_outcome(i, HALF, C, late[i])
            nc.vector.tensor_reduce(
                largest[:, i, :], outcome_pages[i][:].rearrange("p (e u) -> p e u", u=U // E),
                mybir.AxisListType.X, ALU.max,
            )
            if i % 2 == 1:
                gap = keep.tile([P, E], F32, name="gap%d" % (i // 2))
                nc.vector.tensor_tensor(gap[:], largest[:, i - 1, :], largest[:, i, :], ALU.subtract)
                nc.sync.dma_start(out=out[i // 2 * P : (i // 2 + 1) * P, :], in_=gap[:])
